import numpy as np
import ml_dtypes


def mxq(x, axis, fmt="e4m3"):
    dtype, down = {"e4m3": (ml_dtypes.float8_e4m3fn, 7), "e5m2": (ml_dtypes.float8_e5m2, 14)}[fmt]
    v = np.moveaxis(np.asarray(x, np.float32).astype(ml_dtypes.bfloat16).astype(np.float64), axis, -1)
    blocks = v.reshape(v.shape[:-1] + (-1, 32))
    amax = np.abs(blocks).max(-1, keepdims=True)
    byte = np.maximum(np.where(amax > 0, np.frexp(amax)[1] - 1 + 127, 0) - down, 1)
    scale = np.exp2(byte - 127.0)
    codes = (blocks / scale).astype(np.float32).astype(dtype).astype(np.float64)
    return np.moveaxis((codes * scale).reshape(v.shape), -1, axis)


WIDE = False


def mx_kscale(k):
    if not WIDE:
        return np.ones(k)
    levels = np.array([10, -10, 5, -5, 0])
    if k % 512:
        return np.exp2(np.random.permutation(np.resize(levels, k // 32))).repeat(32)
    a = np.empty((k // 512, 16))
    for p in range(k // 512):
        a[p, :8] = np.random.permutation(np.resize(levels, 8))
        for g in range(8):
            far = levels[np.abs(levels - a[p, g]) >= 10]
            a[p, g + 8] = far[np.random.randint(len(far))]
    return np.exp2(a.ravel()).repeat(32)


def f64(x):
    return np.asarray(x).astype(np.float64)


def striped(idx):
    return np.tile(idx.reshape(-1, 16).T, (8, 1)).astype(np.uint16)


def unstriped(offs):
    return offs[:16].T.reshape(-1).astype(np.int64)


def striped8(idx):
    return np.concatenate([x.reshape(-1, 16).T for x in idx]).astype(np.uint16)


def runs(offs, k):
    lists = np.stack([offs[16 * r : 16 * r + 16].T.reshape(-1) for r in range(8)]).astype(np.int64)
    return lists[np.arange(k) % 512 // 64]


def pack_weight(w):
    k, n = w.shape
    w = f64(np.asarray(w, np.float32).astype(ml_dtypes.bfloat16)).reshape(k // 32, 32, n)
    amax = np.abs(w).max(1)
    byte = np.clip(np.where(amax > 0, np.frexp(amax)[1] - 1 + 127 - 7, 1), 1, 254)
    scaled = (w * np.exp2(127.0 - byte)[:, None, :]).reshape(k, n).astype(np.float32)
    words = np.ascontiguousarray(scaled.reshape(k // 512, 128, 4, n).transpose(0, 1, 3, 2)).astype(ml_dtypes.float8_e4m3fn).view(np.uint8)
    return words, np.ascontiguousarray(byte.astype(np.uint8).reshape(k // 512, 16, n))


def unpack_weight(words, scales):
    g, p, n, _ = words.shape
    vals = np.ascontiguousarray(words).view(ml_dtypes.float8_e4m3fn).astype(np.float64) * np.repeat(np.exp2(scales.astype(np.float64) - 127.0), 8, axis=1)[..., None]
    return vals.transpose(0, 1, 3, 2).reshape(g * 512, n)


E2M1 = np.array([0.0, 0.5, 1.0, 1.5, 2.0, 3.0, 4.0, 6.0, -0.0, -0.5, -1.0, -1.5, -2.0, -3.0, -4.0, -6.0])


def pack_fp4(w):
    k, n = w.shape
    w = f64(np.asarray(w, np.float32).astype(ml_dtypes.bfloat16)).reshape(k // 32, 32, n)
    amax = np.abs(w).max(1)
    mant, ex = np.frexp(amax / 6.0)
    byte = np.clip(np.where(amax > 0, np.where(mant > 0.5, ex, ex - 1) + 127, 1), 1, 254)
    scaled = (w * np.exp2(127.0 - byte)[:, None, :]).reshape(k, n).astype(np.float32)
    c = np.ascontiguousarray(scaled.reshape(k // 512, 128, 4, n).transpose(0, 1, 3, 2)).astype(ml_dtypes.float4_e2m1fn).view(np.uint8) & 0xF
    words = (c[..., 0::2] | (c[..., 1::2] << 4)).reshape(k // 512, 128, 2 * n)
    return np.ascontiguousarray(words), np.ascontiguousarray(byte.astype(np.uint8).reshape(k // 512, 16, n))


def unpack_fp4(words, scales):
    g, _, n = scales.shape
    words = np.ascontiguousarray(words).reshape(g, 128, n, 2)
    nib = np.empty((g, 128, n, 4), np.uint8)
    nib[..., 0::2] = words & 0xF
    nib[..., 1::2] = words >> 4
    vals = E2M1[nib] * np.repeat(np.exp2(scales.astype(np.float64) - 127.0), 8, axis=1)[..., None]
    return vals.transpose(0, 1, 3, 2).reshape(g * 512, n)


def sigmoid(v):
    return 1.0 / (1.0 + np.exp(-np.maximum(v, -700.0)))

def planes(y):
    n, m = y.shape
    v = y.astype(np.float32).astype(ml_dtypes.bfloat16).astype(np.float64).reshape(n // 32, 32, m)
    top = np.abs(v).max(1)
    byte = np.clip(np.where(top > 0, np.frexp(top)[1] - 1 + 127 - 7, 1), 1, 254)
    codes = (v * np.exp2(127.0 - byte)[:, None, :]).reshape(n, m).astype(np.float32).astype(ml_dtypes.float8_e4m3fn).view(np.uint8)
    words = codes.reshape(n // 512, 128, 4, m).transpose(0, 1, 3, 2)
    return np.ascontiguousarray(words), np.ascontiguousarray(byte.astype(np.uint8).reshape(n // 512, 16, m))


K, T, S, V, H = 512, 2048, 512, 512, 512


def setup_inputs():
    n = np.random.standard_normal
    s = mx_kscale(K)[:, None]
    u = mx_kscale(S)
    packed_xT = pack_weight(n((K, T)) * s)
    packed_w1 = pack_fp4(n((K, H)) / np.sqrt(K) / s)
    packed_w2 = pack_fp4(n((K, H)) / np.sqrt(K) / s)
    packed_w3 = pack_fp4(n((K, H)) / np.sqrt(K) / s)
    return {
        "x_words": packed_xT[0],
        "x_scales": packed_xT[1],
        "w1_words": packed_w1[0],
        "w1_scales": packed_w1[1],
        "w2_words": packed_w2[0],
        "w2_scales": packed_w2[1],
        "w3_words": packed_w3[0],
        "w3_scales": packed_w3[1],
        "ga": (np.random.uniform(0.5, 1.5, (H, 1)) * u[:, None]).astype(np.float32),
        "gb": (np.random.uniform(0.5, 1.5, (H, 1)) / u[:, None]).astype(np.float32),
        "offs": striped(np.random.permutation(T)[:S]),
        "two": striped(np.random.permutation(T)[:S]),
        "n1": striped8(np.stack([np.random.permutation(S) for _ in range(8)])),
        "n2": striped8(np.stack([np.random.permutation(S) for _ in range(8)])),
        "three": striped(np.random.permutation(T)[:V]),
        "n3": striped8(np.stack([np.random.permutation(V) for _ in range(8)])),
        "n4": striped8(np.stack([np.random.permutation(V) for _ in range(8)])),
        "n5": striped8(np.stack([np.random.permutation(V) for _ in range(8)])),
        "n6": striped8(np.stack([np.random.permutation(V) for _ in range(8)])),
    }


def reference(x_words, x_scales, w1_words, w1_scales, w2_words, w2_scales, w3_words, w3_scales, ga, gb, offs, two, n1, n2, three, n3, n4, n5, n6):
    xq = unpack_weight(x_words, x_scales)[:, unstriped(offs)]
    y = unpack_fp4(w1_words, w1_scales).T @ xq
    x_two = unpack_weight(x_words, x_scales)[:, unstriped(two)]
    d = unpack_fp4(w2_words, w2_scales).T @ x_two
    z = f64(ga) * (y * (sigmoid(d[np.arange(H)[:, None], runs(n2, H)])) - (0.5 * (y[np.arange(H)[:, None], runs(n1, H)])))
    x_three = unpack_weight(x_words, x_scales)[:, unstriped(three)]
    b = unpack_fp4(w3_words, w3_scales).T @ x_three
    z2 = f64(gb) * (np.minimum(np.maximum(b, b[np.arange(H)[:, None], runs(n3, H)]), b[np.arange(H)[:, None], runs(n4, H)]))
    s = 0.0625 * ((mxq(z, 0, "e4m3").T @ mxq(z2, 0, "e4m3")))
    out_0 = (s - (s[np.arange(S)[:, None], runs(n5, S)])) * (sigmoid(s[np.arange(S)[:, None], runs(n6, S)]))
    return (out_0,) + planes(out_0)

@@ -1,0 +1,250 @@
+from contextlib import ExitStack
+
+import concourse.mybir as mybir
+from concourse.masks import make_identity
+
+F32 = mybir.dt.float32
+BF16 = mybir.dt.bfloat16
+I32 = mybir.dt.int32
+U32 = mybir.dt.uint32
+U16 = mybir.dt.uint16
+U8 = mybir.dt.uint8
+FP8X4 = mybir.dt.float8_e4m3fn_x4
+FP4X4 = mybir.dt.float4_e2m1fn_x4
+ALU = mybir.AluOpType
+ACT = mybir.ActivationFunctionType
+
+P = 128
+T = 2048
+N = 512
+PACK = 4
+HALF = N // 2
+FLOPS = 4 * 2 * 512 * 512 * 512
+
+
+def tile_picked_twkgatebminmxgdif_none_po_kernel(
+    tc, x_words, x_scales, w1_words, w1_scales, w2_words, w2_scales, w3_words, w3_scales,
+    ga, gb, offs, two, n1, n2, three, n3, n4, n5, n6, out_0, out_1, out_2,
+):
+    nc = tc.nc
+    with ExitStack() as ctx:
+        lists = ctx.enter_context(tc.tile_pool(name="lists", bufs=1))
+        sb = ctx.enter_context(tc.tile_pool(name="sb", bufs=1))
+        psum = ctx.enter_context(tc.psum_pool(name="psum", bufs=1))
+
+        def load_list(src, name):
+            t = lists.tile([P, N // 16], U16, name=name)
+            nc.sync.dma_start(t[:], src)
+            return t
+
+        def load_scale_rows(dst, src):
+            for q in range(4):
+                nc.sync.dma_start(dst[32 * q : 32 * q + 4, :].bitcast(I32), src[0, 4 * q : 4 * q + 4, :].bitcast(I32))
+
+        def bank(i, name):
+            return psum.tile([P, N], F32, name=name, tag="bank%d" % i)
+
+        def halves(tile_of_offsets, h):
+            return tile_of_offsets[:, h * HALF // 16 : (h + 1) * HALF // 16]
+
+        xs = sb.tile([P, T], U8, name="xs", align_bytes=64)
+        nc.gpsimd.memset(xs[:].bitcast(I32), 0)
+        ws_raw = {}
+        for name in ("w3", "w2", "w1"):
+            ws_raw[name] = sb.tile([P, N], U8, name=name + "s_raw", align_bytes=64)
+            nc.vector.memset(ws_raw[name][:].bitcast(I32), 0)
+        gain_rows = sb.tile([P, P], F32, name="gain_rows")
+        nc.gpsimd.memset(gain_rows[:], 0.0)
+        b_win = [sb.tile([P, 2 * N], F32, name="b_win%d" % t, align_bytes=64) for t in range(PACK)]
+        d_win = [sb.tile([P, N], F32, name="d_win%d" % t, align_bytes=64) for t in range(PACK)]
+        y_win = [sb.tile([P, N], F32, name="y_win%d" % t, align_bytes=64) for t in range(PACK)]
+        for t in range(PACK):
+            nc.vector.memset(b_win[t][:, N:], 0.0)
+        ident = sb.tile([P, P], F32, name="ident")
+        make_identity(nc, ident[:])
+        warm = sb.tile([P, 1], F32, name="warm")
+        nc.scalar.activation(warm[:], b_win[0][:, N : N + 1], ACT.Sigmoid)
+
+        xw = sb.tile([P, T], I32, name="xw", align_bytes=64)
+        nc.sync.dma_start(xw[:], x_words[0].rearrange("p c r -> p (c r)").bitcast(I32))
+        l_three = load_list(three, "l_three")
+        l_two = load_list(two, "l_two")
+        l_offs = load_list(offs, "l_offs")
+        load_scale_rows(xs, x_scales)
+        l_n3 = load_list(n3, "l_n3")
+        l_n4 = load_list(n4, "l_n4")
+        ww_raw = {}
+
+        def load_words(name, words):
+            ww_raw[name] = sb.tile([P, 2 * N], U8, name=name + "w_raw", tag="w2_stage" if name == "w2" else "w_stage", align_bytes=64)
+            nc.sync.dma_start(ww_raw[name][:].bitcast(I32), words[0].bitcast(I32))
+
+        def load_weight(name, words, scales):
+            load_words(name, words)
+            load_scale_rows(ws_raw[name], scales)
+
+        load_words("w3", w3_words)
+        load_scale_rows(ws_raw["w3"], w3_scales)
+        for i, g in ((1, gb), (0, ga)):
+            nc.gpsimd.dma_start(
+                gain_rows[PACK * i : PACK * i + PACK, :].rearrange("t (q r) -> t q r", r=8),
+                g.rearrange("(q t r) o -> t q (r o)", t=PACK, r=8),
+            )
+        load_weight("w2", w2_words, w2_scales)
+        l_n2 = load_list(n2, "l_n2")
+        load_scale_rows(ws_raw["w1"], w1_scales)
+        l_n1 = load_list(n1, "l_n1")
+        l_n5 = load_list(n5, "l_n5")
+        l_n6 = load_list(n6, "l_n6")
+
+        picked_s = {}
+        picked_w = {}
+        order = (("w3", l_three), ("w2", l_two), ("w1", l_offs))
+        for name, offsets in order:
+            picked_w[name] = sb.tile([P, N], I32, name="pw_" + name, align_bytes=64)
+            nc.vector.tensor_copy(picked_w[name][:].bitcast(U32), xw[:].bitcast(U32).indirect(offsets[:]))
+
+        gain_bank = bank(7, "gain_bank")
+        nc.tensor.transpose(gain_bank[:, 0:P], gain_rows[:], ident[:])
+        gains = sb.tile([P, 2 * PACK], F32, name="gains")
+        gb_abs = sb.tile([P, PACK], F32, name="gb_abs")
+        nc.scalar.activation(gb_abs[:], gain_bank[:, PACK : 2 * PACK], ACT.Abs)
+        nc.scalar.copy(gains[:], gain_bank[:, 0 : 2 * PACK])
+        step = sb.tile([P, PACK], F32, name="step")
+        sign = sb.tile([P, PACK], F32, name="sign")
+        ga_signed = sb.tile([P, PACK], F32, name="ga_signed")
+        ga_half = sb.tile([P, PACK], F32, name="ga_half")
+        nc.gpsimd.tensor_scalar(step[:], gains[:, PACK:], 0.0, None, ALU.is_ge)
+        nc.gpsimd.tensor_scalar(sign[:], step[:], 2.0, -1.0, ALU.mult, ALU.add)
+        nc.gpsimd.tensor_tensor(ga_signed[:], gains[:, :PACK], sign[:], ALU.mult)
+        nc.gpsimd.tensor_scalar(ga_half[:], ga_signed[:], -0.5, 0.0, ALU.mult, ALU.add)
+
+        def project(name, offsets, first_bank):
+            ww = sb.tile([P, 2 * N], U8, name=name + "w", align_bytes=64)
+            ws = sb.tile([P, N], U8, name=name + "s", align_bytes=64)
+            picked_s[name] = sb.tile([P, N], U8, name="ps_" + name, align_bytes=64)
+            nc.vector.tensor_copy(picked_s[name][:], xs[:].indirect(offsets[:]))
+            nc.vector.tensor_copy(
+                ww[:].bitcast(I32).rearrange("p (t q i) -> p t q i", t=PACK, i=4),
+                ww_raw[name][:].bitcast(I32).rearrange("p (q t i) -> p t q i", t=PACK, i=4),
+            )
+            nc.vector.tensor_copy(
+                ws[:].bitcast(I32).rearrange("p (t q i) -> p t q i", t=PACK, i=2),
+                ws_raw[name][:].bitcast(I32).rearrange("p (q t i) -> p t q i", t=PACK, i=2),
+            )
+            banks = []
+            for t in range(PACK):
+                acc = bank(first_bank + t, name + "_acc%d" % t)
+                nc.tensor.matmul_mx(
+                    out=acc[:],
+                    lhsT=ww[:, 2 * P * t : 2 * P * (t + 1)].bitcast(FP4X4),
+                    lhsT_scale=ws[:, P * t : P * (t + 1)],
+                    rhs=picked_w[name][:].bitcast(FP8X4),
+                    rhs_scale=picked_s[name][:],
+                    start=True,
+                    stop=True,
+                )
+                banks.append(acc)
+            return banks
+
+        b_acc = project("w3", l_three, 0)
+        load_words("w1", w1_words)
+        b_own = sb.tile([P, PACK, N], BF16, name="b_own", align_bytes=64)
+        for t in range(PACK):
+            nc.scalar.activation(b_win[t][:, :N], b_acc[t][:], ACT.Copy, scale=gb_abs[:, t : t + 1])
+        for t in range(PACK):
+            nc.scalar.activation(b_own[:, t, :], b_acc[t][:], ACT.Copy, scale=gb_abs[:, t : t + 1])
+        d_acc = project("w2", l_two, 4)
+        y_acc = project("w1", l_offs, 0)
+        d_gate = sb.tile([P, PACK, N], F32, name="d_gate", align_bytes=64)
+        for t in range(PACK):
+            nc.scalar.copy(d_win[t][:], d_acc[t][:])
+            for h in range(2):
+                nc.scalar.activation(d_gate[:, t, h * HALF : (h + 1) * HALF], d_win[t][:].indirect(halves(l_n2, h)), ACT.Sigmoid)
+            nc.scalar.activation(y_win[t][:], y_acc[t][:], ACT.Copy, scale=ga_half[:, t : t + 1])
+
+        b_n3 = sb.tile([P, PACK, N], BF16, name="b_n3", align_bytes=64)
+        b_n4 = sb.tile([P, PACK, N], BF16, name="b_n4", align_bytes=64)
+        larger = sb.tile([P, PACK, N], BF16, name="larger", align_bytes=64)
+        z2 = sb.tile([P, PACK, N], BF16, name="z2", align_bytes=64)
+        for t in range(PACK):
+            nc.vector.tensor_copy(b_n3[:, t, :], b_win[t][:].indirect(l_n3[:]))
+            nc.vector.tensor_copy(b_n4[:, t, :], b_win[t][:].indirect(l_n4[:]))
+        nc.vector.tensor_tensor(larger[:], b_n3[:], b_own[:], ALU.max)
+        gated = sb.tile([P, PACK, N], F32, name="gated", align_bytes=64)
+        nc.vector.scalar_tensor_tensor(gated[:, 0, :], y_acc[0][:], ga_signed[:, 0:1], d_gate[:, 0, :], ALU.mult, ALU.mult)
+        nc.vector.tensor_tensor(z2[:], larger[:], b_n4[:], ALU.min)
+        z2_woven = sb.tile([P, N, PACK], BF16, name="z2_woven", align_bytes=64)
+        nc.scalar.copy(
+            z2_woven[:].rearrange("p (c i) t -> p c t i", i=4),
+            z2[:].rearrange("p t (c i) -> p c t i", i=4),
+        )
+
+        for t in range(1, PACK):
+            nc.vector.scalar_tensor_tensor(gated[:, t, :], y_acc[t][:], ga_signed[:, t : t + 1], d_gate[:, t, :], ALU.mult, ALU.mult)
+        z = sb.tile([P, PACK, N], F32, name="z", align_bytes=64)
+        z_woven = sb.tile([P, PACK, P, PACK], BF16, name="z_woven", align_bytes=64)
+        z2_codes = sb.tile([P, N], U32, name="z2_codes", align_bytes=64)
+        z2_scales = sb.tile([P, N], U8, name="z2_scales", align_bytes=64)
+        for h in range(2):
+            cols = slice(h * HALF, (h + 1) * HALF)
+            for t in range(PACK):
+                nc.vector.tensor_tensor(z[:, t, cols], y_win[t][:].indirect(halves(l_n1, h)), gated[:, t, cols], ALU.add)
+            dst = z_woven[:, :, h * P // 2 : (h + 1) * P // 2, :].rearrange("p u (a b) t -> p a t b u", b=2)
+            src = z[:, :, cols].rearrange("p t (a b u) -> p a t b u", b=2, u=PACK)
+            if h == 0:
+                nc.scalar.copy(dst, src)
+            else:
+                nc.vector.quantize_mx(z2_codes[:].bitcast(FP8X4), z2_scales[:], z2_woven[:].rearrange("p c t -> p (c t)"))
+                nc.vector.tensor_copy(dst, src)
+        z_codes = sb.tile([P, N], U32, name="z_codes", align_bytes=64)
+        z_scales = sb.tile([P, N], U8, name="z_scales", align_bytes=64)
+        s_acc = []
+        for u in range(PACK):
+            cols = slice(u * P, (u + 1) * P)
+            nc.vector.quantize_mx(z_codes[:, cols].bitcast(FP8X4), z_scales[:, cols], z_woven[:, u, :, :].rearrange("p m t -> p (m t)"))
+            acc = bank(4 + u, "s_acc%d" % u)
+            nc.tensor.matmul_mx(
+                out=acc[:],
+                lhsT=z_codes[:, cols].bitcast(FP8X4),
+                lhsT_scale=z_scales[:, cols],
+                rhs=z2_codes[:].bitcast(FP8X4),
+                rhs_scale=z2_scales[:],
+                start=True,
+                stop=True,
+            )
+            s_acc.append(acc)
+
+        s_win = d_win
+        s_own = sb.tile([P, PACK, N], F32, name="s_own", align_bytes=64)
+        gate = sb.tile([P, PACK, N], F32, name="gate", align_bytes=64)
+        diff = sb.tile([P, PACK, N], F32, name="diff", align_bytes=64)
+        res = sb.tile([P, PACK, N], F32, name="res", align_bytes=64)
+        res_woven = sb.tile([P, N, PACK], BF16, name="res_woven", align_bytes=64)
+        res_codes = sb.tile([P, N], I32, name="res_codes", align_bytes=64)
+        res_scales = sb.tile([P, N], U8, name="res_scales", align_bytes=64)
+        out_rows = out_0.rearrange("(p u) v -> p u v", u=PACK)
+        out_words = out_1[0].rearrange("p c r -> p (c r)").bitcast(I32)
+        for u in range(PACK):
+            nc.scalar.activation(s_win[u][:], s_acc[u][:], ACT.Copy, scale=0.0625)
+        for h in range(2):
+            cols = slice(h * HALF, (h + 1) * HALF)
+            for u in range(PACK):
+                nc.scalar.activation(gate[:, u, cols], s_win[u][:].indirect(halves(l_n6, h)), ACT.Sigmoid)
+                if h == 0:
+                    nc.vector.tensor_copy(s_own[:, u, :], s_win[u][:])
+                nc.vector.tensor_tensor(diff[:, u, cols], s_win[u][:].indirect(halves(l_n5, h)), s_own[:, u, cols], ALU.subtract)
+            nc.vector.scalar_tensor_tensor(res[:, :, cols], diff[:, :, cols], -1.0, gate[:, :, cols], ALU.mult, ALU.mult)
+            nc.sync.dma_start(out_rows[:, :, cols], res[:, :, cols])
+            dst = res_woven[:, cols, :].rearrange("p (c i) t -> p c t i", i=4)
+            src = res[:, :, cols].rearrange("p t (c i) -> p c t i", i=4)
+            if h == 0:
+                nc.scalar.copy(dst, src)
+            else:
+                nc.vector.tensor_copy(dst, src)
+        for h in range(2):
+            cols = slice(h * HALF, (h + 1) * HALF)
+            nc.vector.quantize_mx(res_codes[:, cols].bitcast(FP8X4), res_scales[:, cols], res_woven[:, cols, :].rearrange("p c t -> p (c t)"))
+            nc.sync.dma_start(out_words[:, cols], res_codes[:, cols])
+        for q in range(4):
+            nc.sync.dma_start(out_2[0, 4 * q : 4 * q + 4, :].bitcast(I32), res_scales[32 * q : 32 * q + 4, :].bitcast(I32))

@@ -50,14 +50,14 @@ def tile_picked_twkgatebminmxgdif_none_po_kernel(
         xs = sb.tile([P, T], U8, name="xs", align_bytes=64)
         nc.gpsimd.memset(xs[:].bitcast(I32), 0)
         ws_raw = {}
-        for name in ("w3", "w2", "w1"):
-            ws_raw[name] = sb.tile([P, N], U8, name=name + "s_raw", align_bytes=64)
+        for name in ("w3", "w1", "w2"):
+            ws_raw[name] = sb.tile([P, N], U8, name=name + "s_raw", tag=name + "s_raw", align_bytes=64)
             nc.vector.memset(ws_raw[name][:].bitcast(I32), 0)
         gain_rows = sb.tile([P, P], F32, name="gain_rows")
         nc.gpsimd.memset(gain_rows[:], 0.0)
         b_win = [sb.tile([P, 2 * N], F32, name="b_win%d" % t, align_bytes=64) for t in range(PACK)]
-        d_win = [sb.tile([P, N], F32, name="d_win%d" % t, align_bytes=64) for t in range(PACK)]
-        y_win = [sb.tile([P, N], F32, name="y_win%d" % t, align_bytes=64) for t in range(PACK)]
+        d_win = [sb.tile([P, N], F32, name="d_win%d" % t, tag="d_win%d" % t, align_bytes=64) for t in range(PACK)]
+        y_win = [sb.tile([P, 2 * N], F32, name="y_win%d" % t, align_bytes=64) for t in range(PACK)]
         for t in range(PACK):
             nc.vector.memset(b_win[t][:, N:], 0.0)
         ident = sb.tile([P, P], F32, name="ident")
@@ -65,18 +65,17 @@ def tile_picked_twkgatebminmxgdif_none_po_kernel(
         warm = sb.tile([P, 1], F32, name="warm")
         nc.scalar.activation(warm[:], b_win[0][:, N : N + 1], ACT.Sigmoid)
 
-        xw = sb.tile([P, T], I32, name="xw", align_bytes=64)
-        nc.sync.dma_start(xw[:], x_words[0].rearrange("p c r -> p (c r)").bitcast(I32))
         l_three = load_list(three, "l_three")
-        l_two = load_list(two, "l_two")
         l_offs = load_list(offs, "l_offs")
+        l_two = load_list(two, "l_two")
         load_scale_rows(xs, x_scales)
         l_n3 = load_list(n3, "l_n3")
-        l_n4 = load_list(n4, "l_n4")
+        xw = sb.tile([P, T], I32, name="xw", align_bytes=64)
+        nc.sync.dma_start(xw[:], x_words[0].rearrange("p c r -> p (c r)").bitcast(I32))
         ww_raw = {}
 
         def load_words(name, words):
-            ww_raw[name] = sb.tile([P, 2 * N], U8, name=name + "w_raw", tag="w2_stage" if name == "w2" else "w_stage", align_bytes=64)
+            ww_raw[name] = sb.tile([P, 2 * N], U8, name=name + "w_raw", align_bytes=64)
             nc.sync.dma_start(ww_raw[name][:].bitcast(I32), words[0].bitcast(I32))
 
         def load_weight(name, words, scales):
@@ -90,40 +89,36 @@ def tile_picked_twkgatebminmxgdif_none_po_kernel(
                 gain_rows[PACK * i : PACK * i + PACK, :].rearrange("t (q r) -> t q r", r=8),
                 g.rearrange("(q t r) o -> t q (r o)", t=PACK, r=8),
             )
+        load_weight("w1", w1_words, w1_scales)
         load_weight("w2", w2_words, w2_scales)
+        l_n4 = load_list(n4, "l_n4")
         l_n2 = load_list(n2, "l_n2")
-        load_scale_rows(ws_raw["w1"], w1_scales)
         l_n1 = load_list(n1, "l_n1")
         l_n5 = load_list(n5, "l_n5")
         l_n6 = load_list(n6, "l_n6")
 
-        picked_s = {}
-        picked_w = {}
-        order = (("w3", l_three), ("w2", l_two), ("w1", l_offs))
-        for name, offsets in order:
-            picked_w[name] = sb.tile([P, N], I32, name="pw_" + name, align_bytes=64)
-            nc.vector.tensor_copy(picked_w[name][:].bitcast(U32), xw[:].bitcast(U32).indirect(offsets[:]))
-
         gain_bank = bank(7, "gain_bank")
         nc.tensor.transpose(gain_bank[:, 0:P], gain_rows[:], ident[:])
-        gains = sb.tile([P, 2 * PACK], F32, name="gains")
         gb_abs = sb.tile([P, PACK], F32, name="gb_abs")
-        nc.scalar.activation(gb_abs[:], gain_bank[:, PACK : 2 * PACK], ACT.Abs)
-        nc.scalar.copy(gains[:], gain_bank[:, 0 : 2 * PACK])
-        step = sb.tile([P, PACK], F32, name="step")
-        sign = sb.tile([P, PACK], F32, name="sign")
-        ga_signed = sb.tile([P, PACK], F32, name="ga_signed")
+        half_sign = sb.tile([P, PACK], F32, name="half_sign")
         ga_half = sb.tile([P, PACK], F32, name="ga_half")
-        nc.gpsimd.tensor_scalar(step[:], gains[:, PACK:], 0.0, None, ALU.is_ge)
-        nc.gpsimd.tensor_scalar(sign[:], step[:], 2.0, -1.0, ALU.mult, ALU.add)
-        nc.gpsimd.tensor_tensor(ga_signed[:], gains[:, :PACK], sign[:], ALU.mult)
-        nc.gpsimd.tensor_scalar(ga_half[:], ga_signed[:], -0.5, 0.0, ALU.mult, ALU.add)
+        nc.scalar.activation(gb_abs[:], gain_bank[:, PACK : 2 * PACK], ACT.Abs)
+        nc.vector.tensor_scalar(half_sign[:], gain_bank[:, PACK : 2 * PACK], 0.0, 0.5, ALU.is_lt, ALU.subtract)
+        nc.vector.tensor_tensor(ga_half[:], gain_bank[:, 0:PACK], half_sign[:], ALU.mult)
 
-        def project(name, offsets, first_bank):
+        def pick_scales(name, offsets):
+            scales = sb.tile([P, N], U8, name="ps_" + name, align_bytes=64)
+            nc.vector.tensor_copy(scales[:], xs[:].indirect(offsets[:]))
+            return scales
+
+        def pick_words(name, offsets, words_tag):
+            words = sb.tile([P, N], I32, name="pw_" + name, tag=words_tag, align_bytes=64)
+            nc.vector.tensor_copy(words[:].bitcast(U32), xw[:].bitcast(U32).indirect(offsets[:]))
+            return words
+
+        def deal(name):
             ww = sb.tile([P, 2 * N], U8, name=name + "w", align_bytes=64)
             ws = sb.tile([P, N], U8, name=name + "s", align_bytes=64)
-            picked_s[name] = sb.tile([P, N], U8, name="ps_" + name, align_bytes=64)
-            nc.vector.tensor_copy(picked_s[name][:], xs[:].indirect(offsets[:]))
             nc.vector.tensor_copy(
                 ww[:].bitcast(I32).rearrange("p (t q i) -> p t q i", t=PACK, i=4),
                 ww_raw[name][:].bitcast(I32).rearrange("p (q t i) -> p t q i", t=PACK, i=4),
@@ -132,70 +127,81 @@ def tile_picked_twkgatebminmxgdif_none_po_kernel(
                 ws[:].bitcast(I32).rearrange("p (t q i) -> p t q i", t=PACK, i=2),
                 ws_raw[name][:].bitcast(I32).rearrange("p (q t i) -> p t q i", t=PACK, i=2),
             )
+            return ww, ws
+
+        def project(name, weight, picked, first_bank):
             banks = []
             for t in range(PACK):
                 acc = bank(first_bank + t, name + "_acc%d" % t)
                 nc.tensor.matmul_mx(
                     out=acc[:],
-                    lhsT=ww[:, 2 * P * t : 2 * P * (t + 1)].bitcast(FP4X4),
-                    lhsT_scale=ws[:, P * t : P * (t + 1)],
-                    rhs=picked_w[name][:].bitcast(FP8X4),
-                    rhs_scale=picked_s[name][:],
+                    lhsT=weight[0][:, 2 * P * t : 2 * P * (t + 1)].bitcast(FP4X4),
+                    lhsT_scale=weight[1][:, P * t : P * (t + 1)],
+                    rhs=picked[0][:].bitcast(FP8X4),
+                    rhs_scale=picked[1][:],
                     start=True,
                     stop=True,
                 )
                 banks.append(acc)
             return banks
 
-        b_acc = project("w3", l_three, 0)
-        load_words("w1", w1_words)
+        s_three = pick_scales("three", l_three)
+        s_offs = pick_scales("offs", l_offs)
+        s_two = pick_scales("two", l_two)
+        x_three = (pick_words("three", l_three, "pw_three"), s_three)
+        b_acc = project("b", deal("w3"), x_three, 0)
+        x_offs = (pick_words("offs", l_offs, "w3s_raw"), s_offs)
+        x_two = (pick_words("two", l_two, "pw_two"), s_two)
+        y_acc = project("y", deal("w1"), x_offs, 4)
+        w2_dealt = deal("w2")
         b_own = sb.tile([P, PACK, N], BF16, name="b_own", align_bytes=64)
         for t in range(PACK):
             nc.scalar.activation(b_win[t][:, :N], b_acc[t][:], ACT.Copy, scale=gb_abs[:, t : t + 1])
         for t in range(PACK):
             nc.scalar.activation(b_own[:, t, :], b_acc[t][:], ACT.Copy, scale=gb_abs[:, t : t + 1])
-        d_acc = project("w2", l_two, 4)
-        y_acc = project("w1", l_offs, 0)
-        d_gate = sb.tile([P, PACK, N], F32, name="d_gate", align_bytes=64)
+        d_acc = project("d", w2_dealt, x_two, 0)
+        for t in range(PACK):
+            nc.scalar.activation(y_win[t][:, :N], y_acc[t][:], ACT.Copy, scale=ga_half[:, t : t + 1])
         for t in range(PACK):
             nc.scalar.copy(d_win[t][:], d_acc[t][:])
             for h in range(2):
-                nc.scalar.activation(d_gate[:, t, h * HALF : (h + 1) * HALF], d_win[t][:].indirect(halves(l_n2, h)), ACT.Sigmoid)
-            nc.scalar.activation(y_win[t][:], y_acc[t][:], ACT.Copy, scale=ga_half[:, t : t + 1])
+                nc.scalar.activation(y_win[t][:, N + h * HALF : N + (h + 1) * HALF], d_win[t][:].indirect(halves(l_n2, h)), ACT.Sigmoid)
 
-        b_n3 = sb.tile([P, PACK, N], BF16, name="b_n3", align_bytes=64)
+        b_n3 = sb.tile([P, PACK, N], BF16, name="b_n3", tag="w2s_raw", align_bytes=64)
         b_n4 = sb.tile([P, PACK, N], BF16, name="b_n4", align_bytes=64)
         larger = sb.tile([P, PACK, N], BF16, name="larger", align_bytes=64)
         z2 = sb.tile([P, PACK, N], BF16, name="z2", align_bytes=64)
         for t in range(PACK):
             nc.vector.tensor_copy(b_n3[:, t, :], b_win[t][:].indirect(l_n3[:]))
+        for t in range(PACK):
             nc.vector.tensor_copy(b_n4[:, t, :], b_win[t][:].indirect(l_n4[:]))
-        nc.vector.tensor_tensor(larger[:], b_n3[:], b_own[:], ALU.max)
-        gated = sb.tile([P, PACK, N], F32, name="gated", align_bytes=64)
-        nc.vector.scalar_tensor_tensor(gated[:, 0, :], y_acc[0][:], ga_signed[:, 0:1], d_gate[:, 0, :], ALU.mult, ALU.mult)
+            if t == PACK - 2:
+                nc.vector.tensor_tensor(larger[:], b_n3[:], b_own[:], ALU.max)
         nc.vector.tensor_tensor(z2[:], larger[:], b_n4[:], ALU.min)
-        z2_woven = sb.tile([P, N, PACK], BF16, name="z2_woven", align_bytes=64)
+        z2_woven = sb.tile([P, N, PACK], BF16, name="z2_woven", tag="d_win3", align_bytes=64)
         nc.scalar.copy(
             z2_woven[:].rearrange("p (c i) t -> p c t i", i=4),
             z2[:].rearrange("p t (c i) -> p c t i", i=4),
         )
 
-        for t in range(1, PACK):
-            nc.vector.scalar_tensor_tensor(gated[:, t, :], y_acc[t][:], ga_signed[:, t : t + 1], d_gate[:, t, :], ALU.mult, ALU.mult)
+        gated = sb.tile([P, PACK, N], F32, name="gated", align_bytes=64)
         z = sb.tile([P, PACK, N], F32, name="z", align_bytes=64)
         z_woven = sb.tile([P, PACK, P, PACK], BF16, name="z_woven", align_bytes=64)
         z2_codes = sb.tile([P, N], U32, name="z2_codes", align_bytes=64)
         z2_scales = sb.tile([P, N], U8, name="z2_scales", align_bytes=64)
+        for t in range(PACK):
+            nc.vector.scalar_tensor_tensor(gated[:, t, :], y_win[t][:, :N], -2.0, y_win[t][:, N:], ALU.mult, ALU.mult)
+        for t in range(PACK - 1):
+            nc.vector.tensor_tensor(z[:, t, :], y_win[t][:].indirect(l_n1[:]), gated[:, t, :], ALU.add)
+        nc.vector.quantize_mx(z2_codes[:].bitcast(FP8X4), z2_scales[:], z2_woven[:].rearrange("p c t -> p (c t)"))
         for h in range(2):
             cols = slice(h * HALF, (h + 1) * HALF)
-            for t in range(PACK):
-                nc.vector.tensor_tensor(z[:, t, cols], y_win[t][:].indirect(halves(l_n1, h)), gated[:, t, cols], ALU.add)
+            nc.vector.tensor_tensor(z[:, PACK - 1, cols], y_win[PACK - 1][:].indirect(halves(l_n1, h)), gated[:, PACK - 1, cols], ALU.add)
             dst = z_woven[:, :, h * P // 2 : (h + 1) * P // 2, :].rearrange("p u (a b) t -> p a t b u", b=2)
             src = z[:, :, cols].rearrange("p t (a b u) -> p a t b u", b=2, u=PACK)
             if h == 0:
                 nc.scalar.copy(dst, src)
             else:
-                nc.vector.quantize_mx(z2_codes[:].bitcast(FP8X4), z2_scales[:], z2_woven[:].rearrange("p c t -> p (c t)"))
                 nc.vector.tensor_copy(dst, src)
         z_codes = sb.tile([P, N], U32, name="z_codes", align_bytes=64)
         z_scales = sb.tile([P, N], U8, name="z_scales", align_bytes=64)
@@ -203,7 +209,7 @@ def tile_picked_twkgatebminmxgdif_none_po_kernel(
         for u in range(PACK):
             cols = slice(u * P, (u + 1) * P)
             nc.vector.quantize_mx(z_codes[:, cols].bitcast(FP8X4), z_scales[:, cols], z_woven[:, u, :, :].rearrange("p m t -> p (m t)"))
-            acc = bank(4 + u, "s_acc%d" % u)
+            acc = bank(u, "s_acc%d" % u)
             nc.tensor.matmul_mx(
                 out=acc[:],
                 lhsT=z_codes[:, cols].bitcast(FP8X4),
@@ -215,7 +221,7 @@ def tile_picked_twkgatebminmxgdif_none_po_kernel(
             )
             s_acc.append(acc)
 
-        s_win = d_win
+        s_win = b_win
         s_own = sb.tile([P, PACK, N], F32, name="s_own", align_bytes=64)
         gate = sb.tile([P, PACK, N], F32, name="gate", align_bytes=64)
         diff = sb.tile([P, PACK, N], F32, name="diff", align_bytes=64)
@@ -226,19 +232,20 @@ def tile_picked_twkgatebminmxgdif_none_po_kernel(
         out_rows = out_0.rearrange("(p u) v -> p u v", u=PACK)
         out_words = out_1[0].rearrange("p c r -> p (c r)").bitcast(I32)
         for u in range(PACK):
-            nc.scalar.activation(s_win[u][:], s_acc[u][:], ACT.Copy, scale=0.0625)
-        for h in range(2):
-            cols = slice(h * HALF, (h + 1) * HALF)
-            for u in range(PACK):
-                nc.scalar.activation(gate[:, u, cols], s_win[u][:].indirect(halves(l_n6, h)), ACT.Sigmoid)
-                if h == 0:
-                    nc.vector.tensor_copy(s_own[:, u, :], s_win[u][:])
-                nc.vector.tensor_tensor(diff[:, u, cols], s_win[u][:].indirect(halves(l_n5, h)), s_own[:, u, cols], ALU.subtract)
+            nc.scalar.activation(s_win[u][:, :N], s_acc[u][:], ACT.Copy, scale=0.0625)
+        for u in range(PACK):
+            nc.scalar.activation(gate[:, u, :], s_win[u][:].indirect(l_n6[:]), ACT.Sigmoid)
+            nc.vector.tensor_copy(s_own[:, u, :], s_win[u][:, :N])
+            nc.vector.tensor_tensor(diff[:, u, :], s_win[u][:].indirect(l_n5[:]), s_own[:, u, :], ALU.subtract)
+        for k in range(4):
+            cols = slice(k * P, (k + 1) * P)
             nc.vector.scalar_tensor_tensor(res[:, :, cols], diff[:, :, cols], -1.0, gate[:, :, cols], ALU.mult, ALU.mult)
-            nc.sync.dma_start(out_rows[:, :, cols], res[:, :, cols])
+            if k % 2 == 1:
+                half = slice((k - 1) * P, (k + 1) * P)
+                nc.sync.dma_start(out_rows[:, :, half], res[:, :, half])
             dst = res_woven[:, cols, :].rearrange("p (c i) t -> p c t i", i=4)
             src = res[:, :, cols].rearrange("p t (c i) -> p c t i", i=4)
-            if h == 0:
+            if k < 3:
                 nc.scalar.copy(dst, src)
             else:
                 nc.vector.tensor_copy(dst, src)

@@ -49,48 +49,47 @@ def tile_picked_twkgatebminmxgdif_none_po_kernel(
 
         xs = sb.tile([P, T], U8, name="xs", align_bytes=64)
         nc.gpsimd.memset(xs[:].bitcast(I32), 0)
-        ws_raw = {}
-        for name in ("w3", "w1", "w2"):
-            ws_raw[name] = sb.tile([P, N], U8, name=name + "s_raw", tag=name + "s_raw", align_bytes=64)
-            nc.vector.memset(ws_raw[name][:].bitcast(I32), 0)
         gain_rows = sb.tile([P, P], F32, name="gain_rows")
         nc.gpsimd.memset(gain_rows[:], 0.0)
+        ws_raw = {}
+        for name in ("w3", "w2", "w1"):
+            ws_raw[name] = sb.tile([P, N], U8, name=name + "s_raw", tag=name + "s_raw", align_bytes=64)
+            nc.vector.memset(ws_raw[name][:].bitcast(I32), 0)
         b_win = [sb.tile([P, 2 * N], F32, name="b_win%d" % t, align_bytes=64) for t in range(PACK)]
         d_win = [sb.tile([P, N], F32, name="d_win%d" % t, tag="d_win%d" % t, align_bytes=64) for t in range(PACK)]
         y_win = [sb.tile([P, 2 * N], F32, name="y_win%d" % t, align_bytes=64) for t in range(PACK)]
         for t in range(PACK):
             nc.vector.memset(b_win[t][:, N:], 0.0)
-        ident = sb.tile([P, P], F32, name="ident")
-        make_identity(nc, ident[:])
         warm = sb.tile([P, 1], F32, name="warm")
         nc.scalar.activation(warm[:], b_win[0][:, N : N + 1], ACT.Sigmoid)
 
-        l_three = load_list(three, "l_three")
-        l_offs = load_list(offs, "l_offs")
-        l_two = load_list(two, "l_two")
-        load_scale_rows(xs, x_scales)
-        l_n3 = load_list(n3, "l_n3")
-        xw = sb.tile([P, T], I32, name="xw", align_bytes=64)
-        nc.sync.dma_start(xw[:], x_words[0].rearrange("p c r -> p (c r)").bitcast(I32))
         ww_raw = {}
 
         def load_words(name, words):
-            ww_raw[name] = sb.tile([P, 2 * N], U8, name=name + "w_raw", align_bytes=64)
+            ww_raw[name] = sb.tile([P, 2 * N], U8, name=name + "w_raw", tag=name + "w_raw", align_bytes=64)
             nc.sync.dma_start(ww_raw[name][:].bitcast(I32), words[0].bitcast(I32))
 
         def load_weight(name, words, scales):
             load_words(name, words)
             load_scale_rows(ws_raw[name], scales)
 
-        load_words("w3", w3_words)
-        load_scale_rows(ws_raw["w3"], w3_scales)
+        l_three = load_list(three, "l_three")
+        l_two = load_list(two, "l_two")
+        l_offs = load_list(offs, "l_offs")
+        load_scale_rows(xs, x_scales)
+        load_weight("w3", w3_words, w3_scales)
+        xw = sb.tile([P, T], I32, name="xw", align_bytes=64)
+        nc.sync.dma_start(xw[:], x_words[0].rearrange("p c r -> p (c r)").bitcast(I32))
         for i, g in ((1, gb), (0, ga)):
             nc.gpsimd.dma_start(
                 gain_rows[PACK * i : PACK * i + PACK, :].rearrange("t (q r) -> t q r", r=8),
                 g.rearrange("(q t r) o -> t q (r o)", t=PACK, r=8),
             )
-        load_weight("w1", w1_words, w1_scales)
+        ident = sb.tile([P, P], F32, name="ident")
+        make_identity(nc, ident[:])
+        l_n3 = load_list(n3, "l_n3")
         load_weight("w2", w2_words, w2_scales)
+        load_weight("w1", w1_words, w1_scales)
         l_n4 = load_list(n4, "l_n4")
         l_n2 = load_list(n2, "l_n2")
         l_n1 = load_list(n1, "l_n1")
@@ -103,8 +102,10 @@ def tile_picked_twkgatebminmxgdif_none_po_kernel(
         half_sign = sb.tile([P, PACK], F32, name="half_sign")
         ga_half = sb.tile([P, PACK], F32, name="ga_half")
         nc.scalar.activation(gb_abs[:], gain_bank[:, PACK : 2 * PACK], ACT.Abs)
-        nc.vector.tensor_scalar(half_sign[:], gain_bank[:, PACK : 2 * PACK], 0.0, 0.5, ALU.is_lt, ALU.subtract)
-        nc.vector.tensor_tensor(ga_half[:], gain_bank[:, 0:PACK], half_sign[:], ALU.mult)
+        gains = sb.tile([P, 2 * PACK], F32, name="gains")
+        nc.scalar.copy(gains[:], gain_bank[:, 0 : 2 * PACK])
+        nc.gpsimd.tensor_scalar(half_sign[:], gains[:, PACK:], 0.0, 0.5, ALU.is_lt, ALU.subtract)
+        nc.gpsimd.tensor_tensor(ga_half[:], gains[:, :PACK], half_sign[:], ALU.mult)
 
         def pick_scales(name, offsets):
             scales = sb.tile([P, N], U8, name="ps_" + name, align_bytes=64)
@@ -116,14 +117,14 @@ def tile_picked_twkgatebminmxgdif_none_po_kernel(
             nc.vector.tensor_copy(words[:].bitcast(U32), xw[:].bitcast(U32).indirect(offsets[:]))
             return words
 
-        def deal(name):
+        def deal(name, engine):
             ww = sb.tile([P, 2 * N], U8, name=name + "w", align_bytes=64)
             ws = sb.tile([P, N], U8, name=name + "s", align_bytes=64)
-            nc.vector.tensor_copy(
+            engine.tensor_copy(
                 ww[:].bitcast(I32).rearrange("p (t q i) -> p t q i", t=PACK, i=4),
                 ww_raw[name][:].bitcast(I32).rearrange("p (q t i) -> p t q i", t=PACK, i=4),
             )
-            nc.vector.tensor_copy(
+            engine.tensor_copy(
                 ws[:].bitcast(I32).rearrange("p (t q i) -> p t q i", t=PACK, i=2),
                 ws_raw[name][:].bitcast(I32).rearrange("p (q t i) -> p t q i", t=PACK, i=2),
             )
@@ -146,28 +147,31 @@ def tile_picked_twkgatebminmxgdif_none_po_kernel(
             return banks
 
         s_three = pick_scales("three", l_three)
-        s_offs = pick_scales("offs", l_offs)
         s_two = pick_scales("two", l_two)
+        s_offs = pick_scales("offs", l_offs)
+        w3_dealt = deal("w3", nc.vector)
         x_three = (pick_words("three", l_three, "pw_three"), s_three)
-        b_acc = project("b", deal("w3"), x_three, 0)
-        x_offs = (pick_words("offs", l_offs, "w3s_raw"), s_offs)
+        b_acc = project("b", w3_dealt, x_three, 0)
         x_two = (pick_words("two", l_two, "pw_two"), s_two)
-        y_acc = project("y", deal("w1"), x_offs, 4)
-        w2_dealt = deal("w2")
-        b_own = sb.tile([P, PACK, N], BF16, name="b_own", align_bytes=64)
+        x_offs = (pick_words("offs", l_offs, "pw_offs"), s_offs)
+        d_acc = project("d", deal("w2", nc.gpsimd), x_two, 4)
+        w1_dealt = deal("w1", nc.gpsimd)
+        b_own = sb.tile([P, PACK, N], BF16, name="b_own", tag="w1s_raw", align_bytes=64)
         for t in range(PACK):
             nc.scalar.activation(b_win[t][:, :N], b_acc[t][:], ACT.Copy, scale=gb_abs[:, t : t + 1])
         for t in range(PACK):
-            nc.scalar.activation(b_own[:, t, :], b_acc[t][:], ACT.Copy, scale=gb_abs[:, t : t + 1])
-        d_acc = project("d", w2_dealt, x_two, 0)
-        for t in range(PACK):
-            nc.scalar.activation(y_win[t][:, :N], y_acc[t][:], ACT.Copy, scale=ga_half[:, t : t + 1])
+            nc.gpsimd.tensor_scalar(b_own[:, t, :], b_win[t][:, :N], 1.0, 0.0, ALU.mult, ALU.add)
+        y_own = sb.tile([P, 2, N], F32, name="y_own", align_bytes=64)
+        y_acc = project("y", w1_dealt, x_offs, 0)
         for t in range(PACK):
             nc.scalar.copy(d_win[t][:], d_acc[t][:])
+            nc.scalar.activation(y_win[t][:, :N], y_acc[t][:], ACT.Copy, scale=ga_half[:, t : t + 1])
             for h in range(2):
                 nc.scalar.activation(y_win[t][:, N + h * HALF : N + (h + 1) * HALF], d_win[t][:].indirect(halves(l_n2, h)), ACT.Sigmoid)
+                if h == 0 and t < 2:
+                    nc.scalar.activation(y_own[:, t, :], y_win[t][:, :N], ACT.Copy, scale=-2.0)
 
-        b_n3 = sb.tile([P, PACK, N], BF16, name="b_n3", tag="w2s_raw", align_bytes=64)
+        b_n3 = sb.tile([P, PACK, N], BF16, name="b_n3", align_bytes=64)
         b_n4 = sb.tile([P, PACK, N], BF16, name="b_n4", align_bytes=64)
         larger = sb.tile([P, PACK, N], BF16, name="larger", align_bytes=64)
         z2 = sb.tile([P, PACK, N], BF16, name="z2", align_bytes=64)
@@ -175,33 +179,38 @@ def tile_picked_twkgatebminmxgdif_none_po_kernel(
             nc.vector.tensor_copy(b_n3[:, t, :], b_win[t][:].indirect(l_n3[:]))
         for t in range(PACK):
             nc.vector.tensor_copy(b_n4[:, t, :], b_win[t][:].indirect(l_n4[:]))
-            if t == PACK - 2:
-                nc.vector.tensor_tensor(larger[:], b_n3[:], b_own[:], ALU.max)
-        nc.vector.tensor_tensor(z2[:], larger[:], b_n4[:], ALU.min)
-        z2_woven = sb.tile([P, N, PACK], BF16, name="z2_woven", tag="d_win3", align_bytes=64)
+        for t in range(0, PACK, 2):
+            nc.vector.tensor_tensor(larger[:, t : t + 2, :], b_n3[:, t : t + 2, :], b_own[:, t : t + 2, :], ALU.max)
+        for t in range(0, PACK, 2):
+            nc.vector.tensor_tensor(z2[:, t : t + 2, :], larger[:, t : t + 2, :], b_n4[:, t : t + 2, :], ALU.min)
+        gated_early = sb.tile([P, 2 * N], F32, name="gated_early", align_bytes=64)
+        late = sb.tile([P, 4 * N], F32, name="late", tag="d_win3", align_bytes=64)
+        gated = [gated_early[:, :N], gated_early[:, N:], late[:, :N], late[:, N : 2 * N]]
+        z2_woven = late[:, 2 * N :].bitcast(BF16)
         nc.scalar.copy(
-            z2_woven[:].rearrange("p (c i) t -> p c t i", i=4),
+            z2_woven.rearrange("p (c i t) -> p c t i", i=4, t=PACK),
             z2[:].rearrange("p t (c i) -> p c t i", i=4),
         )
 
-        gated = sb.tile([P, PACK, N], F32, name="gated", align_bytes=64)
         z = sb.tile([P, PACK, N], F32, name="z", align_bytes=64)
         z_woven = sb.tile([P, PACK, P, PACK], BF16, name="z_woven", align_bytes=64)
         z2_codes = sb.tile([P, N], U32, name="z2_codes", align_bytes=64)
         z2_scales = sb.tile([P, N], U8, name="z2_scales", align_bytes=64)
-        for t in range(PACK):
-            nc.vector.scalar_tensor_tensor(gated[:, t, :], y_win[t][:, :N], -2.0, y_win[t][:, N:], ALU.mult, ALU.mult)
+        for t in range(2):
+            nc.gpsimd.tensor_tensor(gated[t], y_own[:, t, :], y_win[t][:, N:], ALU.mult)
+        for t in range(2, PACK):
+            nc.vector.scalar_tensor_tensor(gated[t], y_win[t][:, :N], -2.0, y_win[t][:, N:], ALU.mult, ALU.mult)
         for t in range(PACK - 1):
-            nc.vector.tensor_tensor(z[:, t, :], y_win[t][:].indirect(l_n1[:]), gated[:, t, :], ALU.add)
-        nc.vector.quantize_mx(z2_codes[:].bitcast(FP8X4), z2_scales[:], z2_woven[:].rearrange("p c t -> p (c t)"))
+            nc.vector.tensor_tensor(z[:, t, :], y_win[t][:].indirect(l_n1[:]), gated[t], ALU.add)
         for h in range(2):
             cols = slice(h * HALF, (h + 1) * HALF)
-            nc.vector.tensor_tensor(z[:, PACK - 1, cols], y_win[PACK - 1][:].indirect(halves(l_n1, h)), gated[:, PACK - 1, cols], ALU.add)
+            nc.vector.tensor_tensor(z[:, PACK - 1, cols], y_win[PACK - 1][:].indirect(halves(l_n1, h)), gated[PACK - 1][:, cols], ALU.add)
             dst = z_woven[:, :, h * P // 2 : (h + 1) * P // 2, :].rearrange("p u (a b) t -> p a t b u", b=2)
             src = z[:, :, cols].rearrange("p t (a b u) -> p a t b u", b=2, u=PACK)
             if h == 0:
                 nc.scalar.copy(dst, src)
             else:
+                nc.vector.quantize_mx(z2_codes[:].bitcast(FP8X4), z2_scales[:], z2_woven)
                 nc.vector.tensor_copy(dst, src)
         z_codes = sb.tile([P, N], U32, name="z_codes", align_bytes=64)
         z_scales = sb.tile([P, N], U8, name="z_scales", align_bytes=64)
@@ -209,7 +218,7 @@ def tile_picked_twkgatebminmxgdif_none_po_kernel(
         for u in range(PACK):
             cols = slice(u * P, (u + 1) * P)
             nc.vector.quantize_mx(z_codes[:, cols].bitcast(FP8X4), z_scales[:, cols], z_woven[:, u, :, :].rearrange("p m t -> p (m t)"))
-            acc = bank(u, "s_acc%d" % u)
+            acc = bank(4 + u, "s_acc%d" % u)
             nc.tensor.matmul_mx(
                 out=acc[:],
                 lhsT=z_codes[:, cols].bitcast(FP8X4),
@@ -233,10 +242,25 @@ def tile_picked_twkgatebminmxgdif_none_po_kernel(
         out_words = out_1[0].rearrange("p c r -> p (c r)").bitcast(I32)
         for u in range(PACK):
             nc.scalar.activation(s_win[u][:, :N], s_acc[u][:], ACT.Copy, scale=0.0625)
-        for u in range(PACK):
+        for u in range(PACK - 1):
             nc.scalar.activation(gate[:, u, :], s_win[u][:].indirect(l_n6[:]), ACT.Sigmoid)
+        for h in range(2):
+            cols = slice(h * HALF, (h + 1) * HALF)
+            nc.scalar.activation(gate[:, PACK - 1, cols], s_win[PACK - 1][:].indirect(halves(l_n6, h)), ACT.Sigmoid)
+        nc.vector.tensor_copy(s_own[:, 0, :], s_win[0][:, :N])
+        nc.vector.tensor_tensor(diff[:, 0, :], s_win[0][:].indirect(l_n5[:]), s_own[:, 0, :], ALU.subtract)
+        for u in range(1, PACK):
             nc.vector.tensor_copy(s_own[:, u, :], s_win[u][:, :N])
+        for u in range(1, PACK - 1):
             nc.vector.tensor_tensor(diff[:, u, :], s_win[u][:].indirect(l_n5[:]), s_own[:, u, :], ALU.subtract)
+        for h in range(2):
+            cols = slice(h * HALF, (h + 1) * HALF)
+            nc.vector.tensor_tensor(diff[:, PACK - 1, cols], s_win[PACK - 1][:].indirect(halves(l_n5, h)), s_own[:, PACK - 1, cols], ALU.subtract)
+
+        def quantize_res(first, end):
+            cols = slice(first, end)
+            nc.vector.quantize_mx(res_codes[:, cols].bitcast(FP8X4), res_scales[:, cols], res_woven[:, cols, :].rearrange("p c t -> p (c t)"))
+
         for k in range(4):
             cols = slice(k * P, (k + 1) * P)
             nc.vector.scalar_tensor_tensor(res[:, :, cols], diff[:, :, cols], -1.0, gate[:, :, cols], ALU.mult, ALU.mult)
@@ -248,10 +272,12 @@ def tile_picked_twkgatebminmxgdif_none_po_kernel(
             if k < 3:
                 nc.scalar.copy(dst, src)
             else:
+                quantize_res(0, HALF)
+                nc.sync.dma_start(out_words[:, :HALF], res_codes[:, :HALF])
                 nc.vector.tensor_copy(dst, src)
-        for h in range(2):
-            cols = slice(h * HALF, (h + 1) * HALF)
-            nc.vector.quantize_mx(res_codes[:, cols].bitcast(FP8X4), res_scales[:, cols], res_woven[:, cols, :].rearrange("p c t -> p (c t)"))
-            nc.sync.dma_start(out_words[:, cols], res_codes[:, cols])
+        quantize_res(HALF, HALF + P)
+        quantize_res(HALF + P, N)
+        nc.sync.dma_start(out_words[:, HALF:], res_codes[:, HALF:])
         for q in range(4):
-            nc.sync.dma_start(out_2[0, 4 * q : 4 * q + 4, :].bitcast(I32), res_scales[32 * q : 32 * q + 4, :].bitcast(I32))
+            queue = nc.sync if q < 2 else nc.scalar
+            queue.dma_start(out_2[0, 4 * q : 4 * q + 4, :].bitcast(I32), res_scales[32 * q : 32 * q + 4, :].bitcast(I32))

from contextlib import ExitStack

import concourse.mybir as mybir
from concourse.masks import make_identity

F32 = mybir.dt.float32
BF16 = mybir.dt.bfloat16
I32 = mybir.dt.int32
U32 = mybir.dt.uint32
U16 = mybir.dt.uint16
U8 = mybir.dt.uint8
FP8X4 = mybir.dt.float8_e4m3fn_x4
FP4X4 = mybir.dt.float4_e2m1fn_x4
ALU = mybir.AluOpType
ACT = mybir.ActivationFunctionType

P = 128
T = 2048
N = 512
PACK = 4
HALF = N // 2
FLOPS = 4 * 2 * 512 * 512 * 512


def tile_picked_twkgatebminmxgdif_none_po_kernel(
    tc, x_words, x_scales, w1_words, w1_scales, w2_words, w2_scales, w3_words, w3_scales,
    ga, gb, offs, two, n1, n2, three, n3, n4, n5, n6, out_0, out_1, out_2,
):
    nc = tc.nc
    with ExitStack() as ctx:
        lists = ctx.enter_context(tc.tile_pool(name="lists", bufs=1))
        sb = ctx.enter_context(tc.tile_pool(name="sb", bufs=1))
        psum = ctx.enter_context(tc.psum_pool(name="psum", bufs=1))

        def load_list(src, name):
            t = lists.tile([P, N // 16], U16, name=name)
            nc.sync.dma_start(t[:], src)
            return t

        def load_scale_rows(dst, src):
            for q in range(4):
                nc.sync.dma_start(dst[32 * q : 32 * q + 4, :].bitcast(I32), src[0, 4 * q : 4 * q + 4, :].bitcast(I32))

        def bank(i, name):
            return psum.tile([P, N], F32, name=name, tag="bank%d" % i)

        def halves(tile_of_offsets, h):
            return tile_of_offsets[:, h * HALF // 16 : (h + 1) * HALF // 16]

        xs = sb.tile([P, T], U8, name="xs", align_bytes=64)
        nc.gpsimd.memset(xs[:].bitcast(I32), 0)
        gain_rows = sb.tile([P, P], F32, name="gain_rows")
        nc.gpsimd.memset(gain_rows[:], 0.0)
        ws_raw = {}
        for name in ("w3", "w2", "w1"):
            ws_raw[name] = sb.tile([P, N], U8, name=name + "s_raw", tag=name + "s_raw", align_bytes=64)
            nc.vector.memset(ws_raw[name][:].bitcast(I32), 0)
        b_win = [sb.tile([P, 2 * N], F32, name="b_win%d" % t, align_bytes=64) for t in range(PACK)]
        d_win = [sb.tile([P, N], F32, name="d_win%d" % t, tag="d_win%d" % t, align_bytes=64) for t in range(PACK)]
        y_win = [sb.tile([P, 2 * N], F32, name="y_win%d" % t, align_bytes=64) for t in range(PACK)]
        for t in range(PACK):
            nc.vector.memset(b_win[t][:, N:], 0.0)
        warm = sb.tile([P, 1], F32, name="warm")
        nc.scalar.activation(warm[:], b_win[0][:, N : N + 1], ACT.Sigmoid)

        ww_raw = {}

        def load_words(name, words):
            ww_raw[name] = sb.tile([P, 2 * N], U8, name=name + "w_raw", tag=name + "w_raw", align_bytes=64)
            nc.sync.dma_start(ww_raw[name][:].bitcast(I32), words[0].bitcast(I32))

        def load_weight(name, words, scales):
            load_words(name, words)
            load_scale_rows(ws_raw[name], scales)

        l_three = load_list(three, "l_three")
        l_two = load_list(two, "l_two")
        l_offs = load_list(offs, "l_offs")
        load_scale_rows(xs, x_scales)
        load_weight("w3", w3_words, w3_scales)
        xw = sb.tile([P, T], I32, name="xw", align_bytes=64)
        nc.sync.dma_start(xw[:], x_words[0].rearrange("p c r -> p (c r)").bitcast(I32))
        for i, g in ((1, gb), (0, ga)):
            nc.gpsimd.dma_start(
                gain_rows[PACK * i : PACK * i + PACK, :].rearrange("t (q r) -> t q r", r=8),
                g.rearrange("(q t r) o -> t q (r o)", t=PACK, r=8),
            )
        ident = sb.tile([P, P], F32, name="ident")
        make_identity(nc, ident[:])
        l_n3 = load_list(n3, "l_n3")
        load_weight("w2", w2_words, w2_scales)
        load_weight("w1", w1_words, w1_scales)
        l_n4 = load_list(n4, "l_n4")
        l_n2 = load_list(n2, "l_n2")
        l_n1 = load_list(n1, "l_n1")
        l_n5 = load_list(n5, "l_n5")
        l_n6 = load_list(n6, "l_n6")

        gain_bank = bank(7, "gain_bank")
        nc.tensor.transpose(gain_bank[:, 0:P], gain_rows[:], ident[:])
        gb_abs = sb.tile([P, PACK], F32, name="gb_abs")
        half_sign = sb.tile([P, PACK], F32, name="half_sign")
        ga_half = sb.tile([P, PACK], F32, name="ga_half")
        nc.scalar.activation(gb_abs[:], gain_bank[:, PACK : 2 * PACK], ACT.Abs)
        gains = sb.tile([P, 2 * PACK], F32, name="gains")
        nc.scalar.copy(gains[:], gain_bank[:, 0 : 2 * PACK])
        nc.gpsimd.tensor_scalar(half_sign[:], gains[:, PACK:], 0.0, 0.5, ALU.is_lt, ALU.subtract)
        nc.gpsimd.tensor_tensor(ga_half[:], gains[:, :PACK], half_sign[:], ALU.mult)

        def pick_scales(name, offsets):
            scales = sb.tile([P, N], U8, name="ps_" + name, align_bytes=64)
            nc.vector.tensor_copy(scales[:], xs[:].indirect(offsets[:]))
            return scales

        def pick_words(name, offsets, words_tag):
            words = sb.tile([P, N], I32, name="pw_" + name, tag=words_tag, align_bytes=64)
            nc.vector.tensor_copy(words[:].bitcast(U32), xw[:].bitcast(U32).indirect(offsets[:]))
            return words

        def deal(name, engine):
            ww = sb.tile([P, 2 * N], U8, name=name + "w", align_bytes=64)
            ws = sb.tile([P, N], U8, name=name + "s", align_bytes=64)
            engine.tensor_copy(
                ww[:].bitcast(I32).rearrange("p (t q i) -> p t q i", t=PACK, i=4),
                ww_raw[name][:].bitcast(I32).rearrange("p (q t i) -> p t q i", t=PACK, i=4),
            )
            engine.tensor_copy(
                ws[:].bitcast(I32).rearrange("p (t q i) -> p t q i", t=PACK, i=2),
                ws_raw[name][:].bitcast(I32).rearrange("p (q t i) -> p t q i", t=PACK, i=2),
            )
            return ww, ws

        def project(name, weight, picked, first_bank):
            banks = []
            for t in range(PACK):
                acc = bank(first_bank + t, name + "_acc%d" % t)
                nc.tensor.matmul_mx(
                    out=acc[:],
                    lhsT=weight[0][:, 2 * P * t : 2 * P * (t + 1)].bitcast(FP4X4),
                    lhsT_scale=weight[1][:, P * t : P * (t + 1)],
                    rhs=picked[0][:].bitcast(FP8X4),
                    rhs_scale=picked[1][:],
                    start=True,
                    stop=True,
                )
                banks.append(acc)
            return banks

        s_three = pick_scales("three", l_three)
        s_two = pick_scales("two", l_two)
        s_offs = pick_scales("offs", l_offs)
        w3_dealt = deal("w3", nc.vector)
        x_three = (pick_words("three", l_three, "pw_three"), s_three)
        b_acc = project("b", w3_dealt, x_three, 0)
        x_two = (pick_words("two", l_two, "pw_two"), s_two)
        x_offs = (pick_words("offs", l_offs, "pw_offs"), s_offs)
        d_acc = project("d", deal("w2", nc.gpsimd), x_two, 4)
        w1_dealt = deal("w1", nc.gpsimd)
        b_own = sb.tile([P, PACK, N], BF16, name="b_own", tag="w1s_raw", align_bytes=64)
        for t in range(PACK):
            nc.scalar.activation(b_win[t][:, :N], b_acc[t][:], ACT.Copy, scale=gb_abs[:, t : t + 1])
        for t in range(PACK):
            nc.gpsimd.tensor_scalar(b_own[:, t, :], b_win[t][:, :N], 1.0, 0.0, ALU.mult, ALU.add)
        y_own = sb.tile([P, 2, N], F32, name="y_own", align_bytes=64)
        y_acc = project("y", w1_dealt, x_offs, 0)
        for t in range(PACK):
            nc.scalar.copy(d_win[t][:], d_acc[t][:])
            nc.scalar.activation(y_win[t][:, :N], y_acc[t][:], ACT.Copy, scale=ga_half[:, t : t + 1])
            for h in range(2):
                nc.scalar.activation(y_win[t][:, N + h * HALF : N + (h + 1) * HALF], d_win[t][:].indirect(halves(l_n2, h)), ACT.Sigmoid)
                if h == 0 and t < 2:
                    nc.scalar.activation(y_own[:, t, :], y_win[t][:, :N], ACT.Copy, scale=-2.0)

        b_n3 = sb.tile([P, PACK, N], BF16, name="b_n3", align_bytes=64)
        b_n4 = sb.tile([P, PACK, N], BF16, name="b_n4", align_bytes=64)
        larger = sb.tile([P, PACK, N], BF16, name="larger", align_bytes=64)
        z2 = sb.tile([P, PACK, N], BF16, name="z2", align_bytes=64)
        for t in range(PACK):
            nc.vector.tensor_copy(b_n3[:, t, :], b_win[t][:].indirect(l_n3[:]))
        for t in range(PACK):
            nc.vector.tensor_copy(b_n4[:, t, :], b_win[t][:].indirect(l_n4[:]))
        for t in range(0, PACK, 2):
            nc.vector.tensor_tensor(larger[:, t : t + 2, :], b_n3[:, t : t + 2, :], b_own[:, t : t + 2, :], ALU.max)
        for t in range(0, PACK, 2):
            nc.vector.tensor_tensor(z2[:, t : t + 2, :], larger[:, t : t + 2, :], b_n4[:, t : t + 2, :], ALU.min)
        gated_early = sb.tile([P, 2 * N], F32, name="gated_early", align_bytes=64)
        late = sb.tile([P, 4 * N], F32, name="late", tag="d_win3", align_bytes=64)
        gated = [gated_early[:, :N], gated_early[:, N:], late[:, :N], late[:, N : 2 * N]]
        z2_woven = late[:, 2 * N :].bitcast(BF16)
        nc.scalar.copy(
            z2_woven.rearrange("p (c i t) -> p c t i", i=4, t=PACK),
            z2[:].rearrange("p t (c i) -> p c t i", i=4),
        )

        z = sb.tile([P, PACK, N], F32, name="z", align_bytes=64)
        z_woven = sb.tile([P, PACK, P, PACK], BF16, name="z_woven", align_bytes=64)
        z2_codes = sb.tile([P, N], U32, name="z2_codes", align_bytes=64)
        z2_scales = sb.tile([P, N], U8, name="z2_scales", align_bytes=64)
        for t in range(2):
            nc.gpsimd.tensor_tensor(gated[t], y_own[:, t, :], y_win[t][:, N:], ALU.mult)
        for t in range(2, PACK):
            nc.vector.scalar_tensor_tensor(gated[t], y_win[t][:, :N], -2.0, y_win[t][:, N:], ALU.mult, ALU.mult)
        for t in range(PACK - 1):
            nc.vector.tensor_tensor(z[:, t, :], y_win[t][:].indirect(l_n1[:]), gated[t], ALU.add)
        for h in range(2):
            cols = slice(h * HALF, (h + 1) * HALF)
            nc.vector.tensor_tensor(z[:, PACK - 1, cols], y_win[PACK - 1][:].indirect(halves(l_n1, h)), gated[PACK - 1][:, cols], ALU.add)
            dst = z_woven[:, :, h * P // 2 : (h + 1) * P // 2, :].rearrange("p u (a b) t -> p a t b u", b=2)
            src = z[:, :, cols].rearrange("p t (a b u) -> p a t b u", b=2, u=PACK)
            if h == 0:
                nc.scalar.copy(dst, src)
            else:
                nc.vector.quantize_mx(z2_codes[:].bitcast(FP8X4), z2_scales[:], z2_woven)
                nc.vector.tensor_copy(dst, src)
        z_codes = sb.tile([P, N], U32, name="z_codes", align_bytes=64)
        z_scales = sb.tile([P, N], U8, name="z_scales", align_bytes=64)
        s_acc = []
        for u in range(PACK):
            cols = slice(u * P, (u + 1) * P)
            nc.vector.quantize_mx(z_codes[:, cols].bitcast(FP8X4), z_scales[:, cols], z_woven[:, u, :, :].rearrange("p m t -> p (m t)"))
            acc = bank(4 + u, "s_acc%d" % u)
            nc.tensor.matmul_mx(
                out=acc[:],
                lhsT=z_codes[:, cols].bitcast(FP8X4),
                lhsT_scale=z_scales[:, cols],
                rhs=z2_codes[:].bitcast(FP8X4),
                rhs_scale=z2_scales[:],
                start=True,
                stop=True,
            )
            s_acc.append(acc)

        s_win = b_win
        s_own = sb.tile([P, PACK, N], F32, name="s_own", align_bytes=64)
        gate = sb.tile([P, PACK, N], F32, name="gate", align_bytes=64)
        diff = sb.tile([P, PACK, N], F32, name="diff", align_bytes=64)
        res = sb.tile([P, PACK, N], F32, name="res", align_bytes=64)
        res_woven = sb.tile([P, N, PACK], BF16, name="res_woven", align_bytes=64)
        res_codes = sb.tile([P, N], I32, name="res_codes", align_bytes=64)
        res_scales = sb.tile([P, N], U8, name="res_scales", align_bytes=64)
        out_rows = out_0.rearrange("(p u) v -> p u v", u=PACK)
        out_words = out_1[0].rearrange("p c r -> p (c r)").bitcast(I32)
        for u in range(PACK):
            nc.scalar.activation(s_win[u][:, :N], s_acc[u][:], ACT.Copy, scale=0.0625)
        for u in range(PACK - 1):
            nc.scalar.activation(gate[:, u, :], s_win[u][:].indirect(l_n6[:]), ACT.Sigmoid)
        for h in range(2):
            cols = slice(h * HALF, (h + 1) * HALF)
            nc.scalar.activation(gate[:, PACK - 1, cols], s_win[PACK - 1][:].indirect(halves(l_n6, h)), ACT.Sigmoid)
        nc.vector.tensor_copy(s_own[:, 0, :], s_win[0][:, :N])
        nc.vector.tensor_tensor(diff[:, 0, :], s_win[0][:].indirect(l_n5[:]), s_own[:, 0, :], ALU.subtract)
        for u in range(1, PACK):
            nc.vector.tensor_copy(s_own[:, u, :], s_win[u][:, :N])
        for u in range(1, PACK - 1):
            nc.vector.tensor_tensor(diff[:, u, :], s_win[u][:].indirect(l_n5[:]), s_own[:, u, :], ALU.subtract)
        for h in range(2):
            cols = slice(h * HALF, (h + 1) * HALF)
            nc.vector.tensor_tensor(diff[:, PACK - 1, cols], s_win[PACK - 1][:].indirect(halves(l_n5, h)), s_own[:, PACK - 1, cols], ALU.subtract)

        def quantize_res(first, end):
            cols = slice(first, end)
            nc.vector.quantize_mx(res_codes[:, cols].bitcast(FP8X4), res_scales[:, cols], res_woven[:, cols, :].rearrange("p c t -> p (c t)"))

        for k in range(4):
            cols = slice(k * P, (k + 1) * P)
            nc.vector.scalar_tensor_tensor(res[:, :, cols], diff[:, :, cols], -1.0, gate[:, :, cols], ALU.mult, ALU.mult)
            if k % 2 == 1:
                half = slice((k - 1) * P, (k + 1) * P)
                nc.sync.dma_start(out_rows[:, :, half], res[:, :, half])
            dst = res_woven[:, cols, :].rearrange("p (c i) t -> p c t i", i=4)
            src = res[:, :, cols].rearrange("p t (c i) -> p c t i", i=4)
            if k < 3:
                nc.scalar.copy(dst, src)
            else:
                quantize_res(0, HALF)
                nc.sync.dma_start(out_words[:, :HALF], res_codes[:, :HALF])
                nc.vector.tensor_copy(dst, src)
        quantize_res(HALF, HALF + P)
        quantize_res(HALF + P, N)
        nc.sync.dma_start(out_words[:, HALF:], res_codes[:, HALF:])
        for q in range(4):
            queue = nc.sync if q < 2 else nc.scalar
            queue.dma_start(out_2[0, 4 * q : 4 * q + 4, :].bitcast(I32), res_scales[32 * q : 32 * q + 4, :].bitcast(I32))
